import numpy as np, ml_dtypes
CORES = [21,109,149,237,277,365,405,493,150,406]
N = 10
NP, TK = 7, 64
def setup_inputs(rng):
    return {"x": rng.standard_normal((N, 128, TK), dtype=np.float32).astype(ml_dtypes.bfloat16), "w1": (rng.standard_normal((N, 128, 128), dtype=np.float32) / 8).astype(ml_dtypes.bfloat16), "w2": (rng.standard_normal((N, 128, NP * 128), dtype=np.float32) / 8).astype(ml_dtypes.bfloat16)}
def setup_inputs_big(rng):
    d = setup_inputs(rng)
    for k in ("x", "w1", "w2"): d[k] = (d[k].astype(np.float32) * 1024.0).astype(d[k].dtype)
    return d
def setup_inputs_small(rng):
    d = setup_inputs(rng)
    for k in ("x", "w1", "w2"): d[k] = (d[k].astype(np.float32) * (1 / 1024.0)).astype(d[k].dtype)
    return d
def setup_inputs_apart(rng):
    d = setup_inputs(rng)
    f = (10.0 ** rng.permutation(np.linspace(-1.5, 1.5, N))).astype(np.float32).reshape(N, 1, 1)
    for k in ("x", "w1", "w2"): d[k] = (d[k].astype(np.float32) * f).astype(d[k].dtype)
    return d
def reference(x, w1, w2):
    X, W1, W2 = x.astype(np.float64), w1.astype(np.float64), w2.astype(np.float64)
    h = [np.maximum(W1[p].T @ X[p], 0.0) for p in range(NP)]
    y = np.full((N, 128, TK), np.nan)
    for q in range(NP, N):
        y[q] = sum(W2[q][:, 128 * p:128 * p + 128].T @ h[p] for p in range(NP))
    return {"y": y.astype(ml_dtypes.bfloat16 if x.dtype != np.float64 else np.float64)}

@@ -1,0 +1,146 @@
+from concourse.bass import DstId, RemoteDMATransfer
+from concourse.mybir import AluOpType
+
+WORLD = 512
+NP, TK, D = 7, 64, 128
+ORDER = [0, 4, 6, 2, 3, 5, 1]
+SLOT = {p: i for i, p in enumerate(ORDER)}
+LANES = 4
+
+SCRATCH = {
+    "xs": ("sbuf", [D, TK], "bfloat16"),
+    "w1s": ("sbuf", [D, D], "bfloat16"),
+    "w2s": ("sbuf", [D, NP * D], "bfloat16"),
+    "zero": ("sbuf", [D, TK], "float32"),
+    "land": ("sbuf", [D, NP * TK], "bfloat16"),
+    "ys": ("sbuf", [D, TK], "bfloat16"),
+    "acc": ("psum", [D, TK], "float32"),
+}
+SEMAPHORES = ["ld", "zs", "mm", "hr", "sent", "cp", "st"] + ["a%d" % p for p in range(NP)]
+
+_CACHE = {}
+
+
+def _plan(T, topo):
+    if "plan" in _CACHE:
+        return _CACHE["plan"]
+    r = list(T.cores)
+
+    def porter(anchor, dsts):
+        for c in range(WORLD):
+            if (topo.host(c) == topo.host(anchor) and topo.chip(c) == topo.chip(anchor) and topo.die(c) == topo.die(anchor)
+                    and c not in r and all(topo.may_write(c, d) for d in dsts)):
+                return c
+        raise ValueError("no porter on the chip of core %d" % anchor)
+
+    pa = porter(r[5], [r[8], r[9]])
+    pc = porter(r[1], [r[8], r[9]])
+    pd = porter(r[4], [r[7], r[9]])
+    plan = {
+        r[0]: [([0], [r[9]]), ([0], [r[8]])],
+        r[1]: [([1], [pc]), ([1], [r[7]])],
+        r[2]: [([2], [pd]), ([2], [r[8]])],
+        r[3]: [([3], [pa]), ([3], [r[5]])],
+        r[4]: [([4], [r[9]]), ([4, 6], [r[8]])],
+        r[5]: [([5], [pa]), ([3, 5], [r[7]])],
+        r[6]: [([6], [r[9]]), ([6], [r[4]])],
+        r[9]: [([0, 4, 6], [r[7]])],
+        pa: [([3, 5], [r[8], r[9]])],
+        pc: [([1], [r[8], r[9]])],
+        pd: [([2], [r[7], r[9]])],
+    }
+    arrive = {}
+    for src, calls in plan.items():
+        for idx, (block, dsts) in enumerate(calls):
+            for a, b in zip(block, block[1:]):
+                if SLOT[b] != SLOT[a] + 1:
+                    raise ValueError("block slots are not neighbours")
+            for d in dsts:
+                if not topo.may_write(src, d):
+                    raise ValueError("core %d may not write to core %d" % (src, d))
+                arrive.setdefault(d, []).append(((src not in r[:NP], idx, len(block)), block))
+    for d in arrive:
+        arrive[d].sort()
+    _CACHE["plan"] = (plan, arrive)
+    return _CACHE["plan"]
+
+
+def _cols(block):
+    return SLOT[block[0]] * TK, (SLOT[block[-1]] + 1) * TK
+
+
+def rank_program(g, core, T, topo):
+    plan, arrive = _plan(T, topo)
+    rank = T.rank_of(core)
+    calls = plan.get(core, [])
+    if rank is None and not calls:
+        return
+    S = T.sem
+    is_p = rank is not None and rank < NP
+    is_q = rank is not None and rank >= NP
+
+    if is_p:
+        g.sync.dma_start(T.xs[:], T.x[:]).then_inc(S.ld, 16)
+        g.scalar.dma_start(T.w1s[:], T.w1[:]).then_inc(S.ld, 16)
+        g.vector.memset(T.zero[:], 0.0).then_inc(S.zs, 1)
+        g.tensor.wait_ge(S.ld, 32)
+        g.tensor.matmul(T.acc[:], T.w1s[:], T.xs[:], start=True, stop=True).then_inc(S.mm, 1)
+        lo, hi = _cols([rank])
+        g.vector.wait_ge(S.zs, 1)
+        g.vector.wait_ge(S.mm, 1)
+        g.vector.tensor_tensor(T.land[:, lo:hi], T.acc[:], T.zero[:], AluOpType.max).then_inc(S.hr, 1)
+    if is_q:
+        half = (NP * D) // 2
+        g.sync.dma_start(T.w2s[:, 0:half], T.w2[:, 0:half]).then_inc(S.ld, 16)
+        g.scalar.dma_start(T.w2s[:, half:], T.w2[:, half:]).then_inc(S.ld, 16)
+
+    here = {}
+    for _, block in arrive.get(core, []):
+        for p in block:
+            here[p] = "a%d" % block[0]
+    if calls:
+        common = None
+        for _, dsts in calls:
+            for d in dsts:
+                common = topo.mask(core, d) if common is None else common & topo.mask(core, d)
+        eng = [i for i in range(common.bit_length()) if (common >> i) & 1]
+        step = len(eng) // LANES
+        sets = [sum(1 << e for e in eng[k::step][:LANES]) for k in range(step)]
+        waited, total = set(), 0
+        for block, dsts in calls:
+            for p in block:
+                name = "hr" if p == rank else here[p]
+                if name not in waited:
+                    g.wait_ge(S[name], 1 if name == "hr" else LANES)
+                    waited.add(name)
+            lo, hi = _cols(block)
+            sem = S["a%d" % block[0]]
+            if len(dsts) == 1:
+                rid, pid = topo.addr(dsts[0], core)
+                g.remote_dma(out_ap=T.land[:, lo:hi], in_ap=T.land[:, lo:hi], remote_sem=sem, local_sem=S.sent,
+                             pid=pid, routing_id=rid, dma_engine_mask=sets[0])
+            else:
+                trs = []
+                for k, d in enumerate(dsts):
+                    rid, pid = topo.addr(d, core)
+                    trs.append(RemoteDMATransfer(dst_ids=[DstId(rid=rid, pnc=pid)], dma_engine_mask=sets[k], remote_sem=sem,
+                                                 src=T.land[:, lo:hi], dst=T.land[:, lo:hi]))
+                g.remote_dma_fused(trs, local_sem=S.sent)
+            total += LANES * len(dsts)
+        g.wait_ge(S.sent, total)
+
+    if is_q:
+        g.tensor.wait_ge(S.ld, 32)
+        done = 0
+        for _, block in arrive[core]:
+            g.tensor.wait_ge(S["a%d" % block[0]], LANES)
+            for p in block:
+                lo, hi = _cols([p])
+                g.tensor.matmul(T.acc[:], T.w2s[:, p * D:(p + 1) * D], T.land[:, lo:hi],
+                                start=(done == 0), stop=(done == NP - 1)).then_inc(S.mm, 1)
+                done += 1
+        g.vector.wait_ge(S.mm, NP)
+        g.vector.tensor_copy(T.ys[:], T.acc[:]).then_inc(S.cp, 1)
+        g.sync.wait_ge(S.cp, 1)
+        g.sync.dma_start(T.y[:], T.ys[:]).then_inc(S.st, 16)
+        g.sync.wait_ge(S.st, 16)

@@ -5,7 +5,6 @@ WORLD = 512
 NP, TK, D = 7, 64, 128
 ORDER = [0, 4, 6, 2, 3, 5, 1]
 SLOT = {p: i for i, p in enumerate(ORDER)}
-LANES = 4
 
 SCRATCH = {
     "xs": ("sbuf", [D, TK], "bfloat16"),
@@ -33,21 +32,24 @@ def _plan(T, topo):
                 return c
         raise ValueError("no porter on the chip of core %d" % anchor)
 
-    pa = porter(r[5], [r[8], r[9]])
-    pc = porter(r[1], [r[8], r[9]])
-    pd = porter(r[4], [r[7], r[9]])
+    q7, q8, q9 = r[NP:]
+    pa = porter(r[5], [q9])
+    pb = porter(r[3], [q8])
+    pc = porter(r[1], [q9])
+    pd = porter(r[4], [q7])
     plan = {
-        r[0]: [([0], [r[9]]), ([0], [r[8]])],
-        r[1]: [([1], [pc]), ([1], [r[7]])],
-        r[2]: [([2], [pd]), ([2], [r[8]])],
-        r[3]: [([3], [pa]), ([3], [r[5]])],
-        r[4]: [([4], [r[9]]), ([4, 6], [r[8]])],
-        r[5]: [([5], [pa]), ([3, 5], [r[7]])],
-        r[6]: [([6], [r[9]]), ([6], [r[4]])],
-        r[9]: [([0, 4, 6], [r[7]])],
-        pa: [([3, 5], [r[8], r[9]])],
-        pc: [([1], [r[8], r[9]])],
-        pd: [([2], [r[7], r[9]])],
+        r[0]: [([0], [(q9, 8)]), ([0], [(q8, 8)]), ([2], [(q9, 8)])],
+        r[1]: [([1], [(pb, 8), (pc, 8)]), ([1], [(q7, 8)])],
+        r[2]: [([2], [(pd, 8)]), ([2], [(r[0], 8), (q8, 8)])],
+        r[3]: [([3], [(pa, 8), (pb, 8)]), ([3], [(r[5], 8)])],
+        r[4]: [([4], [(q9, 8)]), ([4, 6], [(q8, 8)])],
+        r[5]: [([5], [(pb, 8), (pa, 8)]), ([3, 5], [(q7, 8)])],
+        r[6]: [([6], [(q9, 8), (r[4], 8)])],
+        q9: [([0, 4, 6], [(q7, 8)])],
+        pa: [([3, 5], [(q9, 8)])],
+        pb: [([3, 5, 1], [(q8, 8)])],
+        pc: [([1], [(q9, 8)])],
+        pd: [([2], [(q7, 8)])],
     }
     arrive = {}
     for src, calls in plan.items():
@@ -55,10 +57,10 @@ def _plan(T, topo):
             for a, b in zip(block, block[1:]):
                 if SLOT[b] != SLOT[a] + 1:
                     raise ValueError("block slots are not neighbours")
-            for d in dsts:
+            for d, n in dsts:
                 if not topo.may_write(src, d):
                     raise ValueError("core %d may not write to core %d" % (src, d))
-                arrive.setdefault(d, []).append(((src not in r[:NP], idx, len(block)), block))
+                arrive.setdefault(d, []).append(((src not in r[:NP], idx, len(block)), block, n))
     for d in arrive:
         arrive[d].sort()
     _CACHE["plan"] = (plan, arrive)
@@ -67,6 +69,28 @@ def _plan(T, topo):
 
 def _cols(block):
     return SLOT[block[0]] * TK, (SLOT[block[-1]] + 1) * TK
+
+
+def _bits(m):
+    return [i for i in range(m.bit_length()) if (m >> i) & 1]
+
+
+def _masks(core, dsts, base, topo):
+    out, k, taken = {}, 0, 0
+    for d, n in dsts:
+        extra = _bits(topo.mask(core, d) & ~base)
+        if len(dsts) > 1 and len(extra) >= n:
+            pick = extra[0::len(extra) // n][:n]
+        elif n > len(_bits(base)):
+            pick = _bits(topo.mask(core, d))[:n]
+        else:
+            pick = _bits(base)[k::len(_bits(base)) // n][:n]
+            k += 1
+        out[d] = sum(1 << e for e in pick)
+        if out[d] & taken or len(pick) != n:
+            raise ValueError("engine sets of one call overlap")
+        taken |= out[d]
+    return out
 
 
 def rank_program(g, core, T, topo):
@@ -95,45 +119,43 @@ def rank_program(g, core, T, topo):
         g.scalar.dma_start(T.w2s[:, half:], T.w2[:, half:]).then_inc(S.ld, 16)
 
     here = {}
-    for _, block in arrive.get(core, []):
+    for _, block, n in arrive.get(core, []):
         for p in block:
-            here[p] = "a%d" % block[0]
+            here[p] = ("a%d" % block[0], n)
     if calls:
-        common = None
+        base = None
         for _, dsts in calls:
-            for d in dsts:
-                common = topo.mask(core, d) if common is None else common & topo.mask(core, d)
-        eng = [i for i in range(common.bit_length()) if (common >> i) & 1]
-        step = len(eng) // LANES
-        sets = [sum(1 << e for e in eng[k::step][:LANES]) for k in range(step)]
+            for d, _ in dsts:
+                base = topo.mask(core, d) if base is None else base & topo.mask(core, d)
         waited, total = set(), 0
         for block, dsts in calls:
+            masks = _masks(core, dsts, base, topo)
             for p in block:
-                name = "hr" if p == rank else here[p]
+                name, count = ("hr", 1) if p == rank else here[p]
                 if name not in waited:
-                    g.wait_ge(S[name], 1 if name == "hr" else LANES)
+                    g.wait_ge(S[name], count)
                     waited.add(name)
             lo, hi = _cols(block)
             sem = S["a%d" % block[0]]
             if len(dsts) == 1:
-                rid, pid = topo.addr(dsts[0], core)
+                rid, pid = topo.addr(dsts[0][0], core)
                 g.remote_dma(out_ap=T.land[:, lo:hi], in_ap=T.land[:, lo:hi], remote_sem=sem, local_sem=S.sent,
-                             pid=pid, routing_id=rid, dma_engine_mask=sets[0])
+                             pid=pid, routing_id=rid, dma_engine_mask=masks[dsts[0][0]])
             else:
                 trs = []
-                for k, d in enumerate(dsts):
+                for d, n in dsts:
                     rid, pid = topo.addr(d, core)
-                    trs.append(RemoteDMATransfer(dst_ids=[DstId(rid=rid, pnc=pid)], dma_engine_mask=sets[k], remote_sem=sem,
+                    trs.append(RemoteDMATransfer(dst_ids=[DstId(rid=rid, pnc=pid)], dma_engine_mask=masks[d], remote_sem=sem,
                                                  src=T.land[:, lo:hi], dst=T.land[:, lo:hi]))
                 g.remote_dma_fused(trs, local_sem=S.sent)
-            total += LANES * len(dsts)
+            total += sum(n for _, n in dsts)
         g.wait_ge(S.sent, total)
 
     if is_q:
         g.tensor.wait_ge(S.ld, 32)
         done = 0
-        for _, block in arrive[core]:
-            g.tensor.wait_ge(S["a%d" % block[0]], LANES)
+        for _, block, n in arrive[core]:
+            g.tensor.wait_ge(S["a%d" % block[0]], n)
             for p in block:
                 lo, hi = _cols([p])
                 g.tensor.matmul(T.acc[:], T.w2s[:, p * D:(p + 1) * D], T.land[:, lo:hi],

from concourse.bass import DstId, RemoteDMATransfer
from concourse.mybir import AluOpType

WORLD = 512
NP, TK, D = 7, 64, 128
ORDER = [0, 4, 6, 2, 3, 5, 1]
SLOT = {p: i for i, p in enumerate(ORDER)}

SCRATCH = {
    "xs": ("sbuf", [D, TK], "bfloat16"),
    "w1s": ("sbuf", [D, D], "bfloat16"),
    "w2s": ("sbuf", [D, NP * D], "bfloat16"),
    "zero": ("sbuf", [D, TK], "float32"),
    "land": ("sbuf", [D, NP * TK], "bfloat16"),
    "ys": ("sbuf", [D, TK], "bfloat16"),
    "acc": ("psum", [D, TK], "float32"),
}
SEMAPHORES = ["ld", "zs", "mm", "hr", "sent", "cp", "st"] + ["a%d" % p for p in range(NP)]

_CACHE = {}


def _plan(T, topo):
    if "plan" in _CACHE:
        return _CACHE["plan"]
    r = list(T.cores)

    def porter(anchor, dsts):
        for c in range(WORLD):
            if (topo.host(c) == topo.host(anchor) and topo.chip(c) == topo.chip(anchor) and topo.die(c) == topo.die(anchor)
                    and c not in r and all(topo.may_write(c, d) for d in dsts)):
                return c
        raise ValueError("no porter on the chip of core %d" % anchor)

    q7, q8, q9 = r[NP:]
    pa = porter(r[5], [q9])
    pb = porter(r[3], [q8])
    pc = porter(r[1], [q9])
    pd = porter(r[4], [q7])
    plan = {
        r[0]: [([0], [(q9, 8)]), ([0], [(q8, 8)]), ([2], [(q9, 8)])],
        r[1]: [([1], [(pb, 8), (pc, 8)]), ([1], [(q7, 8)])],
        r[2]: [([2], [(pd, 8)]), ([2], [(r[0], 8), (q8, 8)])],
        r[3]: [([3], [(pa, 8), (pb, 8)]), ([3], [(r[5], 8)])],
        r[4]: [([4], [(q9, 8)]), ([4, 6], [(q8, 8)])],
        r[5]: [([5], [(pb, 8), (pa, 8)]), ([3, 5], [(q7, 8)])],
        r[6]: [([6], [(q9, 8), (r[4], 8)])],
        q9: [([0, 4, 6], [(q7, 8)])],
        pa: [([3, 5], [(q9, 8)])],
        pb: [([3, 5, 1], [(q8, 8)])],
        pc: [([1], [(q9, 8)])],
        pd: [([2], [(q7, 8)])],
    }
    arrive = {}
    for src, calls in plan.items():
        for idx, (block, dsts) in enumerate(calls):
            for a, b in zip(block, block[1:]):
                if SLOT[b] != SLOT[a] + 1:
                    raise ValueError("block slots are not neighbours")
            for d, n in dsts:
                if not topo.may_write(src, d):
                    raise ValueError("core %d may not write to core %d" % (src, d))
                arrive.setdefault(d, []).append(((src not in r[:NP], idx, len(block)), block, n))
    for d in arrive:
        arrive[d].sort()
    _CACHE["plan"] = (plan, arrive)
    return _CACHE["plan"]


def _cols(block):
    return SLOT[block[0]] * TK, (SLOT[block[-1]] + 1) * TK


def _bits(m):
    return [i for i in range(m.bit_length()) if (m >> i) & 1]


def _masks(core, dsts, base, topo):
    out, k, taken = {}, 0, 0
    for d, n in dsts:
        extra = _bits(topo.mask(core, d) & ~base)
        if len(dsts) > 1 and len(extra) >= n:
            pick = extra[0::len(extra) // n][:n]
        elif n > len(_bits(base)):
            pick = _bits(topo.mask(core, d))[:n]
        else:
            pick = _bits(base)[k::len(_bits(base)) // n][:n]
            k += 1
        out[d] = sum(1 << e for e in pick)
        if out[d] & taken or len(pick) != n:
            raise ValueError("engine sets of one call overlap")
        taken |= out[d]
    return out


def rank_program(g, core, T, topo):
    plan, arrive = _plan(T, topo)
    rank = T.rank_of(core)
    calls = plan.get(core, [])
    if rank is None and not calls:
        return
    S = T.sem
    is_p = rank is not None and rank < NP
    is_q = rank is not None and rank >= NP

    if is_p:
        g.sync.dma_start(T.xs[:], T.x[:]).then_inc(S.ld, 16)
        g.scalar.dma_start(T.w1s[:], T.w1[:]).then_inc(S.ld, 16)
        g.vector.memset(T.zero[:], 0.0).then_inc(S.zs, 1)
        g.tensor.wait_ge(S.ld, 32)
        g.tensor.matmul(T.acc[:], T.w1s[:], T.xs[:], start=True, stop=True).then_inc(S.mm, 1)
        lo, hi = _cols([rank])
        g.vector.wait_ge(S.zs, 1)
        g.vector.wait_ge(S.mm, 1)
        g.vector.tensor_tensor(T.land[:, lo:hi], T.acc[:], T.zero[:], AluOpType.max).then_inc(S.hr, 1)
    if is_q:
        half = (NP * D) // 2
        g.sync.dma_start(T.w2s[:, 0:half], T.w2[:, 0:half]).then_inc(S.ld, 16)
        g.scalar.dma_start(T.w2s[:, half:], T.w2[:, half:]).then_inc(S.ld, 16)

    here = {}
    for _, block, n in arrive.get(core, []):
        for p in block:
            here[p] = ("a%d" % block[0], n)
    if calls:
        base = None
        for _, dsts in calls:
            for d, _ in dsts:
                base = topo.mask(core, d) if base is None else base & topo.mask(core, d)
        waited, total = set(), 0
        for block, dsts in calls:
            masks = _masks(core, dsts, base, topo)
            for p in block:
                name, count = ("hr", 1) if p == rank else here[p]
                if name not in waited:
                    g.wait_ge(S[name], count)
                    waited.add(name)
            lo, hi = _cols(block)
            sem = S["a%d" % block[0]]
            if len(dsts) == 1:
                rid, pid = topo.addr(dsts[0][0], core)
                g.remote_dma(out_ap=T.land[:, lo:hi], in_ap=T.land[:, lo:hi], remote_sem=sem, local_sem=S.sent,
                             pid=pid, routing_id=rid, dma_engine_mask=masks[dsts[0][0]])
            else:
                trs = []
                for d, n in dsts:
                    rid, pid = topo.addr(d, core)
                    trs.append(RemoteDMATransfer(dst_ids=[DstId(rid=rid, pnc=pid)], dma_engine_mask=masks[d], remote_sem=sem,
                                                 src=T.land[:, lo:hi], dst=T.land[:, lo:hi]))
                g.remote_dma_fused(trs, local_sem=S.sent)
            total += sum(n for _, n in dsts)
        g.wait_ge(S.sent, total)

    if is_q:
        g.tensor.wait_ge(S.ld, 32)
        done = 0
        for _, block, n in arrive[core]:
            g.tensor.wait_ge(S["a%d" % block[0]], n)
            for p in block:
                lo, hi = _cols([p])
                g.tensor.matmul(T.acc[:], T.w2s[:, p * D:(p + 1) * D], T.land[:, lo:hi],
                                start=(done == 0), stop=(done == NP - 1)).then_inc(S.mm, 1)
                done += 1
        g.vector.wait_ge(S.mm, NP)
        g.vector.tensor_copy(T.ys[:], T.acc[:]).then_inc(S.cp, 1)
        g.sync.wait_ge(S.cp, 1)
        g.sync.dma_start(T.y[:], T.ys[:]).then_inc(S.st, 16)
        g.sync.wait_ge(S.st, 16)
